import numpy as np
import ml_dtypes


def mxq(x, axis, fmt="e4m3"):
    dtype, down = {"e4m3": (ml_dtypes.float8_e4m3fn, 7), "e5m2": (ml_dtypes.float8_e5m2, 14)}[fmt]
    v = np.moveaxis(np.asarray(x, np.float32).astype(ml_dtypes.bfloat16).astype(np.float64), axis, -1)
    blocks = v.reshape(v.shape[:-1] + (-1, 32))
    amax = np.abs(blocks).max(-1, keepdims=True)
    byte = np.maximum(np.where(amax > 0, np.frexp(amax)[1] - 1 + 127, 0) - down, 1)
    scale = np.exp2(byte - 127.0)
    codes = (blocks / scale).astype(np.float32).astype(dtype).astype(np.float64)
    return np.moveaxis((codes * scale).reshape(v.shape), -1, axis)


WIDE = False


def mx_kscale(k):
    if not WIDE:
        return np.ones(k)
    levels = np.array([10, -10, 5, -5, 0])
    if k % 512:
        return np.exp2(np.random.permutation(np.resize(levels, k // 32))).repeat(32)
    a = np.empty((k // 512, 16))
    for p in range(k // 512):
        a[p, :8] = np.random.permutation(np.resize(levels, 8))
        for g in range(8):
            far = levels[np.abs(levels - a[p, g]) >= 10]
            a[p, g + 8] = far[np.random.randint(len(far))]
    return np.exp2(a.ravel()).repeat(32)


def f64(x):
    return np.asarray(x).astype(np.float64)


def striped(idx):
    return np.tile(idx.reshape(-1, 16).T, (8, 1)).astype(np.uint16)


def unstriped(offs):
    return offs[:16].T.reshape(-1).astype(np.int64)


E2M1 = np.array([0.0, 0.5, 1.0, 1.5, 2.0, 3.0, 4.0, 6.0, -0.0, -0.5, -1.0, -1.5, -2.0, -3.0, -4.0, -6.0])


def pack_weight(w, fmt):
    k, n = w.shape
    w = f64(np.asarray(w, np.float32).astype(ml_dtypes.bfloat16)).reshape(k // 32, 32, n)
    amax = np.abs(w).max(1)
    if fmt == "e4m3":
        byte = np.frexp(amax)[1] - 1 + 127 - 7
    else:
        mant, ex = np.frexp(amax / 6.0)
        byte = np.where(mant > 0.5, ex, ex - 1) + 127
    byte = np.clip(np.where(amax > 0, byte, 1), 1, 254)
    scaled = (w * np.exp2(127.0 - byte)[:, None, :]).reshape(k, n).astype(np.float32)
    by_word = np.ascontiguousarray(scaled.reshape(k // 512, 128, 4, n).transpose(0, 1, 3, 2))
    if fmt == "e4m3":
        words = by_word.astype(ml_dtypes.float8_e4m3fn).view(np.uint8)
    else:
        c = by_word.astype(ml_dtypes.float4_e2m1fn).view(np.uint8) & 0xF
        words = (c[..., 0::2] | (c[..., 1::2] << 4)).reshape(k // 512, 128, 2 * n)
    return np.ascontiguousarray(words), np.ascontiguousarray(byte.astype(np.uint8).reshape(k // 512, 16, n))


def unpack_weight(words, scales, fmt):
    g, _, n = scales.shape
    words = np.ascontiguousarray(words).reshape(g, 128, n, -1)
    if fmt == "e4m3":
        vals = words.view(ml_dtypes.float8_e4m3fn).astype(np.float64)
    else:
        nib = np.empty((g, 128, n, 4), np.uint8)
        nib[..., 0::2] = words & 0xF
        nib[..., 1::2] = words >> 4
        vals = E2M1[nib]
    vals = vals * np.repeat(np.exp2(scales.astype(np.float64) - 127.0), 8, axis=1)[..., None]
    return vals.transpose(0, 1, 3, 2).reshape(g * 512, n)


def gelu(v):
    return 0.5 * v * (1.0 + np.tanh(np.sqrt(2.0 / np.pi) * (v + 0.044715 * v**3)))


def striped8(idx):
    return np.concatenate([v.reshape(-1, 16).T for v in idx]).astype(np.uint16)


def unstriped8(offs):
    return np.stack([offs[16 * g:16 * g + 16].T.reshape(-1) for g in range(8)]).astype(np.int64)


def heads(h, wgt, idx8):
    r = np.arange(h.shape[0])
    return wgt[r // 4 % 128] * h[r[:, None], idx8[r % 512 // 64]]


def put_heads(h, wgs, idx8, t2):
    r = np.arange(h.shape[0])
    page = np.zeros((h.shape[0], t2))
    page[r[:, None], idx8[r % 512 // 64]] = wgs[r // 4 % 128] * h
    return page


K, T, S, H, T2, P, N = 1024, 2048, 1024, 1024, 2048, 1024, 384

def setup_inputs():
    n = np.random.standard_normal
    s = mx_kscale(K)[:, None]
    u = mx_kscale(H)[:, None]
    d = {}
    d["tab_words"], d["tab_scales"] = pack_weight(n((K, T)) * s, "e4m3")
    d["offs"] = striped(np.random.permutation(T)[:S])
    d["w1"] = (n((K, H)) / s / K ** 0.5).astype(np.float32)
    d["w2_words"], d["w2_scales"] = pack_weight(n((K, H)) / s / K ** 0.5, "e2m1")
    d["gain"] = (1.4 * np.exp(0.3 * n(H)) * np.where(n(H) > 0, 1.0, -1.0)).astype(np.float32)
    d["offs2"] = striped8(np.stack([np.random.permutation(T2)[:S] for _ in range(8)]))
    d["wgs"] = np.repeat(np.random.uniform(0.5, 2.0, (8, S)), 16, axis=0).astype(np.float32)
    d["offs3"] = striped8(np.stack([np.random.permutation(T2)[:P] for _ in range(8)]))
    d["wgt"] = np.repeat(np.random.uniform(0.5, 2.0, (8, P)), 16, axis=0).astype(np.float32)
    d["cold"] = (n((H, P)) * u).astype(np.float32)
    d["w3"] = (1.5 * n((H, N)) / u / H ** 0.5).astype(np.float32)
    return d

def reference(tab_words, tab_scales, offs, w1, w2_words, w2_scales, gain, offs2, wgs, offs3, wgt, cold, w3):
    v = unpack_weight(tab_words, tab_scales, "e4m3")[:, unstriped(offs)]
    a = mxq(f64(w1), 0, "e4m3").T @ v
    b = unpack_weight(w2_words, w2_scales, "e2m1").T @ v
    h = f64(gain)[:, None] * np.maximum(a, b)
    page = put_heads(h, f64(wgs), unstriped8(offs2), T2)
    x = heads(page, f64(wgt), unstriped8(offs3))
    z = f64(cold) / (1.0 + np.exp(-x))
    out = mxq(f64(w3), 0, "e4m3").T @ mxq(z, 0, "e4m3")
    return out

@@ -1,0 +1,307 @@
+from contextlib import ExitStack
+
+import concourse.mybir as mybir
+
+K, T, S, H, T2, M, N = 1024, 2048, 1024, 1024, 2048, 1024, 384
+FLOPS = 2 * (2 * K * H * S + H * N * M)
+
+F32 = mybir.dt.float32
+BF16 = mybir.dt.bfloat16
+I32 = mybir.dt.int32
+U32 = mybir.dt.uint32
+U16 = mybir.dt.uint16
+U8 = mybir.dt.uint8
+FP8X4 = mybir.dt.float8_e4m3fn_x4
+FP4X4 = mybir.dt.float4_e2m1fn_x4
+ALU = mybir.AluOpType
+ACT = mybir.ActivationFunctionType
+
+P = 128
+BANK = 512
+TAIL = 256
+
+FUSE_SCATTER = True
+FUSE_GATHER = True
+ZMUL_POOL = False
+TAIL_INTER_SCALAR = (0, 1)
+
+
+def tile_list_vase_life_scores_kernel(
+    tc, tab_words, tab_scales, offs, w1, w2_words, w2_scales, gain, offs2, wgs, offs3, wgt, cold, w3, out
+):
+    nc = tc.nc
+    with ExitStack() as ctx:
+        keep = ctx.enter_context(tc.tile_pool(name="keep", bufs=1))
+        ring = ctx.enter_context(tc.tile_pool(name="ring", bufs=2))
+        psum = ctx.enter_context(tc.psum_pool(name="psum", bufs=8))
+
+        o1 = keep.tile([P, S // 16], U16, name="o1")
+        o2 = keep.tile([P, S // 16], U16, name="o2")
+        o3 = keep.tile([P, M // 16], U16, name="o3")
+        tabs = keep.tile([P, 2, T], U8, name="tabs")
+        w2s_raw = keep.tile([P, 2, H], U8, name="w2s_raw")
+        page = keep.tile([P, T2], F32, name="page")
+        gain_sb = keep.tile([P, 2, 4], F32, name="gain_sb")
+
+        nc.gpsimd.memset(tabs[:].rearrange("p a t -> p (a t)").bitcast(I32), 0)
+        nc.vector.memset(w2s_raw[:].rearrange("p a t -> p (a t)").bitcast(I32), 0)
+
+        def load_w1(b):
+            raws = {}
+            for a in range(2):
+                for hf in range(2):
+                    raw = ring.tile([P, 4, 256], F32, name="w1raw", bufs=4)
+                    nc.sync.dma_start(
+                        out=raw[:],
+                        in_=w1[512 * a : 512 * (a + 1), 512 * b + 256 * hf : 512 * b + 256 * (hf + 1)].rearrange(
+                            "(p j) c -> p j c", j=4
+                        ),
+                    )
+                    raws[a, hf] = raw
+            return raws
+
+        w1q = {}
+        w1s = {}
+
+        def quant_w1(b, raws):
+            for a in range(2):
+                grp = ring.tile([P, 4, P, 4], BF16, name="w1grp", align_bytes=64)
+                for hf in range(2):
+                    nc.scalar.copy(
+                        out=grp[:, :, 64 * hf : 64 * (hf + 1), :].rearrange("p t m j -> p m j t"),
+                        in_=raws[a, hf][:].rearrange("p j (m t) -> p m j t", t=4),
+                    )
+                w1q[b, a] = keep.tile([P, 512], U32, name=f"w1q{b}{a}", align_bytes=64)
+                w1s[b, a] = keep.tile([P, 512], U8, name=f"w1s{b}{a}", align_bytes=64)
+                nc.vector.quantize_mx(
+                    out=w1q[b, a][:].bitcast(FP8X4),
+                    scales=w1s[b, a][:],
+                    in_=grp[:].rearrange("p t m j -> p (t m j)"),
+                )
+
+        nc.sync.dma_start(o1[:], offs)
+        raws0 = load_w1(0)
+        for q in range(4):
+            nc.gpsimd.dma_start(
+                out=tabs[32 * q : 32 * q + 4, :, :].bitcast(I32),
+                in_=tab_scales[:, 4 * q : 4 * q + 4, :].rearrange("a r t -> r a t").bitcast(I32),
+            )
+        for q in range(4):
+            nc.gpsimd.dma_start(
+                out=w2s_raw[32 * q : 32 * q + 4, :, :].bitcast(I32),
+                in_=w2_scales[:, 4 * q : 4 * q + 4, :].rearrange("a r t -> r a t").bitcast(I32),
+            )
+        nc.gpsimd.dma_start(out=gain_sb[:], in_=gain.rearrange("(b p i) -> p b i", b=2, i=4))
+        w2w_raw = keep.tile([P, 2, 2 * H], U8, name="w2w_raw")
+        nc.sync.dma_start(out=w2w_raw[:].bitcast(I32), in_=w2_words.rearrange("a p c -> p a c").bitcast(I32))
+        tabw = []
+        for a in range(2):
+            tw = keep.tile([P, T], U32, name=f"tabw{a}")
+            nc.sync.dma_start(out=tw[:].bitcast(I32), in_=tab_words[a].rearrange("p t i -> p (t i)").bitcast(I32))
+            tabw.append(tw)
+        wgs_sb = keep.tile([P, S], F32, name="wgs_sb")
+        nc.sync.dma_start(out=wgs_sb[:], in_=wgs)
+        nc.sync.dma_start(o2[:], offs2)
+        nc.sync.dma_start(o3[:], offs3)
+        wgt_sb = keep.tile([P, M], F32, name="wgt_sb")
+        nc.sync.dma_start(out=wgt_sb[:], in_=wgt)
+
+        gs = {}
+
+        def gather_scales(hf):
+            for a in range(2):
+                gs[a, hf] = keep.tile([P, BANK], U8, name=f"gs{a}{hf}", align_bytes=64)
+                nc.vector.tensor_copy(gs[a, hf][:], tabs[:, a, :].indirect(o1[:, 32 * hf : 32 * (hf + 1)]))
+
+        gather_scales(0)
+        quant_w1(0, raws0)
+
+        w2w = {}
+        w2s = {}
+
+        def deal_w2(b):
+            w2w[b] = keep.tile([P, 2, 4, 2 * P], U8, name=f"w2w{b}", align_bytes=64)
+            nc.scalar.copy(
+                out=w2w[b][:].bitcast(U16).rearrange("p a t m -> p a m t"),
+                in_=w2w_raw[:, :, 1024 * b : 1024 * (b + 1)].bitcast(U16).rearrange("p a (m t) -> p a m t", t=4),
+            )
+            w2s[b] = keep.tile([P, 2, 4, P], U8, name=f"w2s{b}", align_bytes=64)
+            nc.gpsimd.tensor_copy(
+                out=w2s[b][:],
+                in_=w2s_raw[:, :, 512 * b : 512 * (b + 1)].rearrange("p a (m t) -> p a t m", t=4),
+            )
+
+        deal_w2(0)
+        nc.gpsimd.memset(page[:], 0.0)
+
+        gw = {}
+        for hf in range(2):
+            if hf == 1:
+                gather_scales(1)
+            for a in range(2):
+                gw[a, hf] = keep.tile([P, BANK], U32, name=f"gw{a}{hf}", align_bytes=64)
+                nc.vector.tensor_copy(gw[a, hf][:], tabw[a][:].indirect(o1[:, 32 * hf : 32 * (hf + 1)]))
+
+        hs = {}
+
+        def stage1(s):
+            b, t = divmod(s, 4)
+            wg = ring.tile([P, S], F32, name="wg")
+            nc.scalar.activation(out=wg[:], in_=wgs_sb[:], func=ACT.Copy, scale=gain_sb[:, b, t : t + 1])
+            mh = ring.tile([P, S], F32, name="mh")
+            for hf in range(2):
+                cols = slice(BANK * hf, BANK * (hf + 1))
+                acc_b = psum.tile([P, BANK], F32, name="bank")
+                for a in range(2):
+                    nc.tensor.matmul_mx(
+                        out=acc_b[:],
+                        lhsT=w2w[b][:, a, t, :].bitcast(FP4X4),
+                        lhsT_scale=w2s[b][:, a, t, :],
+                        rhs=gw[a, hf][:].bitcast(FP8X4),
+                        rhs_scale=gs[a, hf][:],
+                        start=(a == 0),
+                        stop=(a == 1),
+                    )
+                acc_a = psum.tile([P, BANK], F32, name="bank")
+                for a in range(2):
+                    nc.tensor.matmul_mx(
+                        out=acc_a[:],
+                        lhsT=w1q[b, a][:, P * t : P * (t + 1)].bitcast(FP8X4),
+                        lhsT_scale=w1s[b, a][:, P * t : P * (t + 1)],
+                        rhs=gw[a, hf][:].bitcast(FP8X4),
+                        rhs_scale=gs[a, hf][:],
+                        start=(a == 0),
+                        stop=(a == 1),
+                    )
+                b_sb = ring.tile([P, BANK], F32, name="b_sb", bufs=4)
+                nc.scalar.copy(out=b_sb[:], in_=acc_b[:])
+                nc.vector.tensor_tensor(mh[:, cols], acc_a[:], b_sb[:], ALU.max)
+            if not FUSE_SCATTER:
+                pieces = 2 if s == 0 else 1
+                for c in range(pieces):
+                    cols = slice(S // pieces * c, S // pieces * (c + 1))
+                    nc.gpsimd.tensor_tensor(mh[:, cols], mh[:, cols], wg[:, cols], ALU.mult)
+            hs[s] = (mh, wg)
+
+        def scatter(s):
+            mh, wg = hs[s]
+            pieces = 2 if s == 0 else 1
+            for c in range(pieces):
+                w = S // pieces
+                cols = slice(w * c, w * (c + 1))
+                window = page[:].indirect(o2[:, w // 16 * c : w // 16 * (c + 1)])
+                if FUSE_SCATTER:
+                    nc.vector.tensor_tensor(window, mh[:, cols], wg[:, cols], ALU.mult)
+                else:
+                    nc.vector.tensor_copy(window, mh[:, cols])
+
+        colds = {}
+
+        def load_cold(s):
+            b, t = divmod(s, 4)
+            colds[s] = ring.tile([P, M], F32, name="cold_sb", bufs=3)
+            nc.sync.dma_start(
+                out=colds[s][:], in_=cold[512 * b : 512 * (b + 1), :].rearrange("(p i) m -> p i m", i=4)[:, t, :]
+            )
+
+        zb = [keep.tile([P, 4, M], BF16, name=f"zb{b}") for b in range(2)]
+
+        def read_page(s, x, sig, cols, last):
+            b, t = divmod(s, 4)
+            window = page[:].indirect(o3[:, cols.start // 16 : cols.stop // 16])
+            if FUSE_GATHER or last:
+                nc.vector.tensor_tensor(x[:, cols], window, wgt_sb[:, cols], ALU.mult)
+            else:
+                nc.vector.tensor_copy(x[:, cols], window)
+                nc.gpsimd.tensor_tensor(x[:, cols], x[:, cols], wgt_sb[:, cols], ALU.mult)
+            nc.scalar.activation(out=sig[:, cols], in_=x[:, cols], func=ACT.Sigmoid)
+
+        def weigh(s, sig, cols, last):
+            b, t = divmod(s, 4)
+            eng = nc.gpsimd if (ZMUL_POOL and not last) else nc.vector
+            eng.tensor_tensor(zb[b][:, t, cols], sig[:, cols], colds[s][:, cols], ALU.mult)
+
+        zq = {}
+
+        def quant_z(b, cols, on_scalar):
+            w = cols.stop - cols.start
+            zi = ring.tile([P, w, 4], BF16, name="zi", align_bytes=64)
+            dst = zi[:].rearrange("p (c i) t -> p c t i", i=4)
+            src = zb[b][:, :, cols].rearrange("p t (c i) -> p c t i", i=4)
+            if on_scalar:
+                nc.scalar.copy(out=dst, in_=src)
+            else:
+                nc.vector.tensor_copy(out=dst, in_=src)
+            codes = keep.tile([P, w], U32, name=f"zq{b}_{cols.start}", align_bytes=64)
+            scales = keep.tile([P, w], U8, name=f"zs{b}_{cols.start}", align_bytes=64)
+            nc.vector.quantize_mx(
+                out=codes[:].bitcast(FP8X4), scales=scales[:], in_=zi[:].rearrange("p c t -> p (c t)")
+            )
+            for c0 in range(cols.start, cols.stop, TAIL):
+                rel = slice(c0 - cols.start, c0 - cols.start + TAIL)
+                zq[b, c0] = (codes[:, rel], scales[:, rel])
+
+        w3q = {}
+        w3s = {}
+
+        def prep_w3(b):
+            raw = ring.tile([P, 4, N], F32, name="w3raw")
+            nc.sync.dma_start(out=raw[:], in_=w3[512 * b : 512 * (b + 1), :].rearrange("(p j) n -> p j n", j=4))
+            grp = ring.tile([P, N, 4], BF16, name="w3grp", align_bytes=64)
+            nc.scalar.copy(
+                out=grp[:].rearrange("p (c i) t -> p c t i", i=4),
+                in_=raw[:].rearrange("p t (c i) -> p c t i", i=4),
+            )
+            w3q[b] = keep.tile([P, N], U32, name=f"w3q{b}", align_bytes=64)
+            w3s[b] = keep.tile([P, N], U8, name=f"w3s{b}", align_bytes=64)
+            nc.vector.quantize_mx(
+                out=w3q[b][:].bitcast(FP8X4), scales=w3s[b][:], in_=grp[:].rearrange("p c t -> p (c t)")
+            )
+
+        def score(c0):
+            staged = ring.tile([P, 3, TAIL], F32, name="staged", bufs=3)
+            banks = [psum.tile([P, BANK], F32, name="bank") for u in range(2)]
+            for n in range(3):
+                for b in range(2):
+                    nc.tensor.matmul_mx(
+                        out=banks[n // 2][:, TAIL * (n % 2) : TAIL * (n % 2 + 1)],
+                        lhsT=w3q[b][:, P * n : P * (n + 1)].bitcast(FP8X4),
+                        lhsT_scale=w3s[b][:, P * n : P * (n + 1)],
+                        rhs=zq[b, c0][0].bitcast(FP8X4),
+                        rhs_scale=zq[b, c0][1],
+                        start=(b == 0),
+                        stop=(b == 1),
+                    )
+            nc.scalar.copy(out=staged[:, 0:2, :].rearrange("p n m -> p (n m)"), in_=banks[0][:])
+            nc.vector.tensor_copy(out=staged[:, 2, :], in_=banks[1][:, 0:TAIL])
+            nc.sync.dma_start(out=out.rearrange("(n p) m -> p n m", p=P)[:, :, c0 : c0 + TAIL], in_=staged[:])
+
+        stage1(0)
+        load_cold(0)
+        raws1 = load_w1(1)
+        for s in range(8):
+            if s == 1:
+                quant_w1(1, raws1)
+                deal_w2(1)
+            if s + 1 < 8:
+                load_cold(s + 1)
+                stage1(s + 1)
+            if s in (2, 3):
+                prep_w3(s - 2)
+            scatter(s)
+            x = ring.tile([P, M], F32, name="x")
+            sig = ring.tile([P, M], F32, name="sig")
+            if s < 7:
+                read_page(s, x, sig, slice(0, M), False)
+                weigh(s, sig, slice(0, M), False)
+            else:
+                for c0 in range(0, M, TAIL):
+                    read_page(s, x, sig, slice(c0, c0 + TAIL), True)
+                for c0 in range(0, M, TAIL):
+                    weigh(s, sig, slice(c0, c0 + TAIL), True)
+                    quant_z(1, slice(c0, c0 + TAIL), c0 // TAIL in TAIL_INTER_SCALAR)
+                for c0 in range(0, M, TAIL):
+                    score(c0)
+            if s == 4:
+                for c0 in range(0, M, BANK):
+                    quant_z(0, slice(c0, c0 + BANK), True)

@@ -20,9 +20,9 @@ P = 128
 BANK = 512
 TAIL = 256
 
-FUSE_SCATTER = True
-FUSE_GATHER = True
-ZMUL_POOL = False
+FUSE_SCATTER = False
+FUSE_GATHER = False
+ZMUL_POOL = True
 TAIL_INTER_SCALAR = (0, 1)
 
 
@@ -43,14 +43,16 @@ def tile_list_vase_life_scores_kernel(
         page = keep.tile([P, T2], F32, name="page")
         gain_sb = keep.tile([P, 2, 4], F32, name="gain_sb")
 
-        nc.gpsimd.memset(tabs[:].rearrange("p a t -> p (a t)").bitcast(I32), 0)
-        nc.vector.memset(w2s_raw[:].rearrange("p a t -> p (a t)").bitcast(I32), 0)
+        nc.vector.memset(tabs[:].rearrange("p a t -> p (a t)").bitcast(I32), 0)
+        nc.gpsimd.memset(w2s_raw[:].rearrange("p a t -> p (a t)").bitcast(I32), 0)
+
+        nc.vector.memset(page[:], 0.0)
 
         def load_w1(b):
             raws = {}
             for a in range(2):
                 for hf in range(2):
-                    raw = ring.tile([P, 4, 256], F32, name="w1raw", bufs=4)
+                    raw = ring.tile([P, 4, 256], F32, name="w1raw", bufs=8)
                     nc.sync.dma_start(
                         out=raw[:],
                         in_=w1[512 * a : 512 * (a + 1), 512 * b + 256 * hf : 512 * b + 256 * (hf + 1)].rearrange(
@@ -79,27 +81,27 @@ def tile_list_vase_life_scores_kernel(
                     in_=grp[:].rearrange("p t m j -> p (t m j)"),
                 )
 
-        nc.sync.dma_start(o1[:], offs)
-        raws0 = load_w1(0)
-        for q in range(4):
-            nc.gpsimd.dma_start(
-                out=tabs[32 * q : 32 * q + 4, :, :].bitcast(I32),
-                in_=tab_scales[:, 4 * q : 4 * q + 4, :].rearrange("a r t -> r a t").bitcast(I32),
-            )
         for q in range(4):
             nc.gpsimd.dma_start(
                 out=w2s_raw[32 * q : 32 * q + 4, :, :].bitcast(I32),
                 in_=w2_scales[:, 4 * q : 4 * q + 4, :].rearrange("a r t -> r a t").bitcast(I32),
             )
-        nc.gpsimd.dma_start(out=gain_sb[:], in_=gain.rearrange("(b p i) -> p b i", b=2, i=4))
-        w2w_raw = keep.tile([P, 2, 2 * H], U8, name="w2w_raw")
-        nc.sync.dma_start(out=w2w_raw[:].bitcast(I32), in_=w2_words.rearrange("a p c -> p a c").bitcast(I32))
+        nc.sync.dma_start(o1[:], offs)
         tabw = []
         for a in range(2):
             tw = keep.tile([P, T], U32, name=f"tabw{a}")
             nc.sync.dma_start(out=tw[:].bitcast(I32), in_=tab_words[a].rearrange("p t i -> p (t i)").bitcast(I32))
             tabw.append(tw)
+        for q in range(4):
+            nc.sync.dma_start(
+                out=tabs[32 * q : 32 * q + 4, :, :].bitcast(I32),
+                in_=tab_scales[:, 4 * q : 4 * q + 4, :].rearrange("a r t -> r a t").bitcast(I32),
+            )
+        w2w_raw = keep.tile([P, 2, 2 * H], U8, name="w2w_raw")
+        nc.sync.dma_start(out=w2w_raw[:].bitcast(I32), in_=w2_words.rearrange("a p c -> p a c").bitcast(I32))
+        raws0 = load_w1(0)
         wgs_sb = keep.tile([P, S], F32, name="wgs_sb")
+        nc.sync.dma_start(out=gain_sb[:], in_=gain.rearrange("(b p i) -> p b i", b=2, i=4))
         nc.sync.dma_start(out=wgs_sb[:], in_=wgs)
         nc.sync.dma_start(o2[:], offs2)
         nc.sync.dma_start(o3[:], offs3)
@@ -113,8 +115,6 @@ def tile_list_vase_life_scores_kernel(
                 gs[a, hf] = keep.tile([P, BANK], U8, name=f"gs{a}{hf}", align_bytes=64)
                 nc.vector.tensor_copy(gs[a, hf][:], tabs[:, a, :].indirect(o1[:, 32 * hf : 32 * (hf + 1)]))
 
-        gather_scales(0)
-        quant_w1(0, raws0)
 
         w2w = {}
         w2s = {}
@@ -125,30 +125,32 @@ def tile_list_vase_life_scores_kernel(
                 out=w2w[b][:].bitcast(U16).rearrange("p a t m -> p a m t"),
                 in_=w2w_raw[:, :, 1024 * b : 1024 * (b + 1)].bitcast(U16).rearrange("p a (m t) -> p a m t", t=4),
             )
-            w2s[b] = keep.tile([P, 2, 4, P], U8, name=f"w2s{b}", align_bytes=64)
-            nc.gpsimd.tensor_copy(
-                out=w2s[b][:],
-                in_=w2s_raw[:, :, 512 * b : 512 * (b + 1)].rearrange("p a (m t) -> p a t m", t=4),
-            )
+
+        def deal_w2_scales(b):
+            for t in range(4):
+                w2s[b, t] = keep.tile([P, 2, P], U8, name=f"w2s{b}{t}", align_bytes=64)
+                nc.gpsimd.tensor_copy(out=w2s[b, t][:], in_=w2s_raw[:, :, 512 * b + t : 512 * (b + 1) : 4])
 
         deal_w2(0)
-        nc.gpsimd.memset(page[:], 0.0)
+        deal_w2_scales(0)
 
         gw = {}
         for hf in range(2):
-            if hf == 1:
-                gather_scales(1)
             for a in range(2):
                 gw[a, hf] = keep.tile([P, BANK], U32, name=f"gw{a}{hf}", align_bytes=64)
                 nc.vector.tensor_copy(gw[a, hf][:], tabw[a][:].indirect(o1[:, 32 * hf : 32 * (hf + 1)]))
+            gather_scales(hf)
+            if hf == 0:
+                quant_w1(0, raws0)
 
         hs = {}
 
         def stage1(s):
             b, t = divmod(s, 4)
-            wg = ring.tile([P, S], F32, name="wg")
+            wg = keep.tile([P, S], F32, name=f"wg{s % 2}")
             nc.scalar.activation(out=wg[:], in_=wgs_sb[:], func=ACT.Copy, scale=gain_sb[:, b, t : t + 1])
-            mh = ring.tile([P, S], F32, name="mh")
+            mh = ring.tile([P, S], F32, name="mh", bufs=3)
+            b_sb = keep.tile([P, S], F32, name=f"bx{s % 2}")
             for hf in range(2):
                 cols = slice(BANK * hf, BANK * (hf + 1))
                 acc_b = psum.tile([P, BANK], F32, name="bank")
@@ -156,7 +158,7 @@ def tile_list_vase_life_scores_kernel(
                     nc.tensor.matmul_mx(
                         out=acc_b[:],
                         lhsT=w2w[b][:, a, t, :].bitcast(FP4X4),
-                        lhsT_scale=w2s[b][:, a, t, :],
+                        lhsT_scale=w2s[b, t][:, a, :],
                         rhs=gw[a, hf][:].bitcast(FP8X4),
                         rhs_scale=gs[a, hf][:],
                         start=(a == 0),
@@ -173,14 +175,10 @@ def tile_list_vase_life_scores_kernel(
                         start=(a == 0),
                         stop=(a == 1),
                     )
-                b_sb = ring.tile([P, BANK], F32, name="b_sb", bufs=4)
-                nc.scalar.copy(out=b_sb[:], in_=acc_b[:])
-                nc.vector.tensor_tensor(mh[:, cols], acc_a[:], b_sb[:], ALU.max)
-            if not FUSE_SCATTER:
-                pieces = 2 if s == 0 else 1
-                for c in range(pieces):
-                    cols = slice(S // pieces * c, S // pieces * (c + 1))
-                    nc.gpsimd.tensor_tensor(mh[:, cols], mh[:, cols], wg[:, cols], ALU.mult)
+                nc.scalar.copy(out=b_sb[:, cols], in_=acc_b[:])
+                nc.vector.tensor_tensor(mh[:, cols], acc_a[:], b_sb[:, cols], ALU.max)
+            if not FUSE_SCATTER and s > 0:
+                nc.gpsimd.tensor_tensor(mh[:], mh[:], wg[:], ALU.mult)
             hs[s] = (mh, wg)
 
         def scatter(s):
@@ -190,7 +188,7 @@ def tile_list_vase_life_scores_kernel(
                 w = S // pieces
                 cols = slice(w * c, w * (c + 1))
                 window = page[:].indirect(o2[:, w // 16 * c : w // 16 * (c + 1)])
-                if FUSE_SCATTER:
+                if FUSE_SCATTER or s == 0:
                     nc.vector.tensor_tensor(window, mh[:, cols], wg[:, cols], ALU.mult)
                 else:
                     nc.vector.tensor_copy(window, mh[:, cols])
@@ -213,7 +211,9 @@ def tile_list_vase_life_scores_kernel(
                 nc.vector.tensor_tensor(x[:, cols], window, wgt_sb[:, cols], ALU.mult)
             else:
                 nc.vector.tensor_copy(x[:, cols], window)
-                nc.gpsimd.tensor_tensor(x[:, cols], x[:, cols], wgt_sb[:, cols], ALU.mult)
+                picked = x
+                x = keep.tile([P, M], F32, name=f"wg{(s + 1) % 2}")
+                nc.gpsimd.tensor_tensor(x[:, cols], picked[:, cols], wgt_sb[:, cols], ALU.mult)
             nc.scalar.activation(out=sig[:, cols], in_=x[:, cols], func=ACT.Sigmoid)
 
         def weigh(s, sig, cols, last):
@@ -245,7 +245,7 @@ def tile_list_vase_life_scores_kernel(
         w3s = {}
 
         def prep_w3(b):
-            raw = ring.tile([P, 4, N], F32, name="w3raw")
+            raw = keep.tile([P, 4, N], F32, name=("w3raw", "sig")[b])
             nc.sync.dma_start(out=raw[:], in_=w3[512 * b : 512 * (b + 1), :].rearrange("(p j) n -> p j n", j=4))
             grp = ring.tile([P, N, 4], BF16, name="w3grp", align_bytes=64)
             nc.scalar.copy(
@@ -276,21 +276,22 @@ def tile_list_vase_life_scores_kernel(
             nc.vector.tensor_copy(out=staged[:, 2, :], in_=banks[1][:, 0:TAIL])
             nc.sync.dma_start(out=out.rearrange("(n p) m -> p n m", p=P)[:, :, c0 : c0 + TAIL], in_=staged[:])
 
-        stage1(0)
-        load_cold(0)
         raws1 = load_w1(1)
+        stage1(0)
+        stage1(1)
         for s in range(8):
-            if s == 1:
+            if s + 2 < 8:
+                stage1(s + 2)
+            scatter(s)
+            if s == 0:
                 quant_w1(1, raws1)
                 deal_w2(1)
-            if s + 1 < 8:
-                load_cold(s + 1)
-                stage1(s + 1)
-            if s in (2, 3):
-                prep_w3(s - 2)
-            scatter(s)
-            x = ring.tile([P, M], F32, name="x")
-            sig = ring.tile([P, M], F32, name="sig")
+                deal_w2_scales(1)
+                prep_w3(0)
+                prep_w3(1)
+            load_cold(s)
+            x = keep.tile([P, M], F32, name=f"bx{s % 2}")
+            sig = keep.tile([P, M], F32, name="sig")
             if s < 7:
                 read_page(s, x, sig, slice(0, M), False)
                 weigh(s, sig, slice(0, M), False)

@@ -21,9 +21,11 @@ BANK = 512
 TAIL = 256
 
 FUSE_SCATTER = False
-FUSE_GATHER = False
+FUSE_GATHER = True
 ZMUL_POOL = True
-TAIL_INTER_SCALAR = (0, 1)
+TAIL_PAIR_SCALAR = (0, 1, 2)
+H_TAG = ("h0", "hsB", "hsA", "hsB", "hsA", "hsC", "hsA", "hsC")
+SIG_TAG = ("hsA", "hsB", "hsA", "hsC", "hsA", "hsC", "hsD", "hsC")
 
 
 def tile_list_vase_life_scores_kernel(
@@ -66,6 +68,7 @@ def tile_list_vase_life_scores_kernel(
         w1s = {}
 
         def quant_w1(b, raws):
+            codes = keep.tile([P, 2, 512], U32, name=("w1q0", "h0")[b], align_bytes=64)
             for a in range(2):
                 grp = ring.tile([P, 4, P, 4], BF16, name="w1grp", align_bytes=64)
                 for hf in range(2):
@@ -73,10 +76,10 @@ def tile_list_vase_life_scores_kernel(
                         out=grp[:, :, 64 * hf : 64 * (hf + 1), :].rearrange("p t m j -> p m j t"),
                         in_=raws[a, hf][:].rearrange("p j (m t) -> p m j t", t=4),
                     )
-                w1q[b, a] = keep.tile([P, 512], U32, name=f"w1q{b}{a}", align_bytes=64)
+                w1q[b, a] = codes[:, a, :]
                 w1s[b, a] = keep.tile([P, 512], U8, name=f"w1s{b}{a}", align_bytes=64)
                 nc.vector.quantize_mx(
-                    out=w1q[b, a][:].bitcast(FP8X4),
+                    out=w1q[b, a].bitcast(FP8X4),
                     scales=w1s[b, a][:],
                     in_=grp[:].rearrange("p t m j -> p (t m j)"),
                 )
@@ -104,9 +107,7 @@ def tile_list_vase_life_scores_kernel(
         nc.sync.dma_start(out=gain_sb[:], in_=gain.rearrange("(b p i) -> p b i", b=2, i=4))
         nc.sync.dma_start(out=wgs_sb[:], in_=wgs)
         nc.sync.dma_start(o2[:], offs2)
-        nc.sync.dma_start(o3[:], offs3)
         wgt_sb = keep.tile([P, M], F32, name="wgt_sb")
-        nc.sync.dma_start(out=wgt_sb[:], in_=wgt)
 
         gs = {}
 
@@ -127,9 +128,10 @@ def tile_list_vase_life_scores_kernel(
             )
 
         def deal_w2_scales(b):
+            dealt = keep.tile([P, 4, 2, P], U8, name=("w2s0", "m0")[b], align_bytes=64)
             for t in range(4):
-                w2s[b, t] = keep.tile([P, 2, P], U8, name=f"w2s{b}{t}", align_bytes=64)
-                nc.gpsimd.tensor_copy(out=w2s[b, t][:], in_=w2s_raw[:, :, 512 * b + t : 512 * (b + 1) : 4])
+                w2s[b, t] = dealt[:, t, :, :]
+                nc.gpsimd.tensor_copy(out=w2s[b, t], in_=w2s_raw[:, :, 512 * b + t : 512 * (b + 1) : 4])
 
         deal_w2(0)
         deal_w2_scales(0)
@@ -149,7 +151,10 @@ def tile_list_vase_life_scores_kernel(
             b, t = divmod(s, 4)
             wg = keep.tile([P, S], F32, name=f"wg{s % 2}")
             nc.scalar.activation(out=wg[:], in_=wgs_sb[:], func=ACT.Copy, scale=gain_sb[:, b, t : t + 1])
-            mh = ring.tile([P, S], F32, name="mh", bufs=3)
+            if s == 0:
+                mh = keep.tile([P, S], F32, name="m0", align_bytes=64)
+            else:
+                mh = ring.tile([P, S], F32, name="mh")
             b_sb = keep.tile([P, S], F32, name=f"bx{s % 2}")
             for hf in range(2):
                 cols = slice(BANK * hf, BANK * (hf + 1))
@@ -177,27 +182,28 @@ def tile_list_vase_life_scores_kernel(
                     )
                 nc.scalar.copy(out=b_sb[:, cols], in_=acc_b[:])
                 nc.vector.tensor_tensor(mh[:, cols], acc_a[:], b_sb[:, cols], ALU.max)
-            if not FUSE_SCATTER and s > 0:
-                nc.gpsimd.tensor_tensor(mh[:], mh[:], wg[:], ALU.mult)
             hs[s] = (mh, wg)
 
-        def scatter(s):
+        def place_product(s):
             mh, wg = hs[s]
-            pieces = 2 if s == 0 else 1
-            for c in range(pieces):
-                w = S // pieces
-                cols = slice(w * c, w * (c + 1))
-                window = page[:].indirect(o2[:, w // 16 * c : w // 16 * (c + 1)])
-                if FUSE_SCATTER or s == 0:
-                    nc.vector.tensor_tensor(window, mh[:, cols], wg[:, cols], ALU.mult)
-                else:
-                    nc.vector.tensor_copy(window, mh[:, cols])
+            h = keep.tile([P, S], F32, name=H_TAG[s], align_bytes=64)
+            width = BANK if s == 0 else S
+            for c0 in range(0, S, width):
+                cols = slice(c0, c0 + width)
+                nc.gpsimd.tensor_tensor(h[:, cols], mh[:, cols], wg[:, cols], ALU.mult)
+            hs[s] = h
+
+        def scatter(s):
+            width = BANK if s == 0 else S
+            for c0 in range(0, S, width):
+                window = page[:].indirect(o2[:, c0 // 16 : (c0 + width) // 16])
+                nc.vector.tensor_copy(window, hs[s][:, c0 : c0 + width])
 
         colds = {}
 
         def load_cold(s):
             b, t = divmod(s, 4)
-            colds[s] = ring.tile([P, M], F32, name="cold_sb", bufs=3)
+            colds[s] = ring.tile([P, M], F32, name="cold_sb", bufs=2)
             nc.sync.dma_start(
                 out=colds[s][:], in_=cold[512 * b : 512 * (b + 1), :].rearrange("(p i) m -> p i m", i=4)[:, t, :]
             )
@@ -223,7 +229,7 @@ def tile_list_vase_life_scores_kernel(
 
         zq = {}
 
-        def quant_z(b, cols, on_scalar):
+        def quant_z(b, cols, on_scalar, codes0):
             w = cols.stop - cols.start
             zi = ring.tile([P, w, 4], BF16, name="zi", align_bytes=64)
             dst = zi[:].rearrange("p (c i) t -> p c t i", i=4)
@@ -232,77 +238,124 @@ def tile_list_vase_life_scores_kernel(
                 nc.scalar.copy(out=dst, in_=src)
             else:
                 nc.vector.tensor_copy(out=dst, in_=src)
-            codes = keep.tile([P, w], U32, name=f"zq{b}_{cols.start}", align_bytes=64)
+            codes = codes0[:, cols]
             scales = keep.tile([P, w], U8, name=f"zs{b}_{cols.start}", align_bytes=64)
             nc.vector.quantize_mx(
-                out=codes[:].bitcast(FP8X4), scales=scales[:], in_=zi[:].rearrange("p c t -> p (c t)")
+                out=codes.bitcast(FP8X4), scales=scales[:], in_=zi[:].rearrange("p c t -> p (c t)")
             )
             for c0 in range(cols.start, cols.stop, TAIL):
                 rel = slice(c0 - cols.start, c0 - cols.start + TAIL)
                 zq[b, c0] = (codes[:, rel], scales[:, rel])
 
+        zi1 = {}
+
+        def pair_copy(c0, first, on_scalar):
+            dst = zi1[c0][:, :, first : first + 2].rearrange("p (c i) t -> p c t i", i=4)
+            src = zb[1][:, first : first + 2, c0 : c0 + TAIL].rearrange("p t (c i) -> p c t i", i=4)
+            if on_scalar:
+                nc.scalar.copy(out=dst, in_=src)
+            else:
+                nc.vector.tensor_copy(out=dst, in_=src)
+
+        def quant_tail(c0):
+            codes = keep.tile([P, TAIL], U32, name=f"zq1_{c0}", align_bytes=64)
+            scales = keep.tile([P, TAIL], U8, name=f"zs1_{c0}", align_bytes=64)
+            nc.vector.quantize_mx(
+                out=codes[:].bitcast(FP8X4), scales=scales[:], in_=zi1[c0][:].rearrange("p c t -> p (c t)")
+            )
+            zq[1, c0] = (codes[:], scales[:])
+
+        w3g = {}
         w3q = {}
         w3s = {}
 
         def prep_w3(b):
-            raw = keep.tile([P, 4, N], F32, name=("w3raw", "sig")[b])
+            raw = ring.tile([P, 4, N], F32, name="w3raw")
             nc.sync.dma_start(out=raw[:], in_=w3[512 * b : 512 * (b + 1), :].rearrange("(p j) n -> p j n", j=4))
             grp = ring.tile([P, N, 4], BF16, name="w3grp", align_bytes=64)
             nc.scalar.copy(
                 out=grp[:].rearrange("p (c i) t -> p c t i", i=4),
                 in_=raw[:].rearrange("p t (c i) -> p c t i", i=4),
             )
-            w3q[b] = keep.tile([P, N], U32, name=f"w3q{b}", align_bytes=64)
-            w3s[b] = keep.tile([P, N], U8, name=f"w3s{b}", align_bytes=64)
-            nc.vector.quantize_mx(
-                out=w3q[b][:].bitcast(FP8X4), scales=w3s[b][:], in_=grp[:].rearrange("p c t -> p (c t)")
-            )
+            w3g[b] = grp
 
-        def score(c0):
-            staged = ring.tile([P, 3, TAIL], F32, name="staged", bufs=3)
-            banks = [psum.tile([P, BANK], F32, name="bank") for u in range(2)]
+        def quant_w3():
+            codes = keep.tile([P, 2, N], U32, name="hsB", align_bytes=64)
+            for b in range(2):
+                w3q[b] = codes[:, b, :]
+                w3s[b] = keep.tile([P, N], U8, name=f"w3s{b}", align_bytes=64)
+                nc.vector.quantize_mx(
+                    out=w3q[b].bitcast(FP8X4), scales=w3s[b][:], in_=w3g[b][:].rearrange("p c t -> p (c t)")
+                )
+
+        banks = {}
+
+        def score_pass(b, c0):
+            if b == 0:
+                banks[c0] = [psum.tile([P, BANK], F32, name="bank") for u in range(2)]
             for n in range(3):
-                for b in range(2):
-                    nc.tensor.matmul_mx(
-                        out=banks[n // 2][:, TAIL * (n % 2) : TAIL * (n % 2 + 1)],
-                        lhsT=w3q[b][:, P * n : P * (n + 1)].bitcast(FP8X4),
-                        lhsT_scale=w3s[b][:, P * n : P * (n + 1)],
-                        rhs=zq[b, c0][0].bitcast(FP8X4),
-                        rhs_scale=zq[b, c0][1],
-                        start=(b == 0),
-                        stop=(b == 1),
-                    )
-            nc.scalar.copy(out=staged[:, 0:2, :].rearrange("p n m -> p (n m)"), in_=banks[0][:])
-            nc.vector.tensor_copy(out=staged[:, 2, :], in_=banks[1][:, 0:TAIL])
+                nc.tensor.matmul_mx(
+                    out=banks[c0][n // 2][:, TAIL * (n % 2) : TAIL * (n % 2 + 1)],
+                    lhsT=w3q[b][:, P * n : P * (n + 1)].bitcast(FP8X4),
+                    lhsT_scale=w3s[b][:, P * n : P * (n + 1)],
+                    rhs=zq[b, c0][0].bitcast(FP8X4),
+                    rhs_scale=zq[b, c0][1],
+                    start=(b == 0 and n != 1),
+                    stop=(b == 1 and n != 0),
+                )
+
+        def store(c0):
+            staged = ring.tile([P, 3, TAIL], F32, name="w1raw", bufs=8)
+            nc.scalar.copy(out=staged[:, 0:2, :].rearrange("p n m -> p (n m)"), in_=banks[c0][0][:])
+            if c0 + TAIL < M:
+                nc.scalar.copy(out=staged[:, 2, :], in_=banks[c0][1][:, 0:TAIL])
+            else:
+                nc.vector.tensor_copy(out=staged[:, 2, :], in_=banks[c0][1][:, 0:TAIL])
             nc.sync.dma_start(out=out.rearrange("(n p) m -> p n m", p=P)[:, :, c0 : c0 + TAIL], in_=staged[:])
 
         raws1 = load_w1(1)
-        stage1(0)
-        stage1(1)
+        nc.sync.dma_start(o3[:], offs3)
+        nc.sync.dma_start(out=wgt_sb[:], in_=wgt)
+        for s in range(2):
+            stage1(s)
+            place_product(s)
+        deal_w2_scales(1)
+        chunks = range(0, M, TAIL)
         for s in range(8):
-            if s + 2 < 8:
-                stage1(s + 2)
             scatter(s)
             if s == 0:
                 quant_w1(1, raws1)
                 deal_w2(1)
-                deal_w2_scales(1)
                 prep_w3(0)
                 prep_w3(1)
+            if s == 3:
+                quant_w3()
+            if s == 6:
+                codes0 = keep.tile([P, M], U32, name="hsA", align_bytes=64)
+                for c0 in range(0, M, BANK):
+                    quant_z(0, slice(c0, c0 + BANK), True, codes0)
+                for c0 in chunks:
+                    zi1[c0] = keep.tile([P, TAIL, 4], BF16, name=f"zi1_{c0}", align_bytes=64)
+                    pair_copy(c0, 0, True)
+            if s + 2 < 8:
+                stage1(s + 2)
             load_cold(s)
             x = keep.tile([P, M], F32, name=f"bx{s % 2}")
-            sig = keep.tile([P, M], F32, name="sig")
+            sig = keep.tile([P, M], F32, name=SIG_TAG[s], align_bytes=64)
             if s < 7:
                 read_page(s, x, sig, slice(0, M), False)
                 weigh(s, sig, slice(0, M), False)
             else:
-                for c0 in range(0, M, TAIL):
-                    read_page(s, x, sig, slice(c0, c0 + TAIL), True)
-                for c0 in range(0, M, TAIL):
+                for c0 in chunks:
+                    score_pass(0, c0)
+                read_page(s, x, sig, slice(0, TAIL), True)
+                for c0 in chunks:
+                    if c0 + TAIL < M:
+                        read_page(s, x, sig, slice(c0 + TAIL, c0 + 2 * TAIL), True)
                     weigh(s, sig, slice(c0, c0 + TAIL), True)
-                    quant_z(1, slice(c0, c0 + TAIL), c0 // TAIL in TAIL_INTER_SCALAR)
-                for c0 in range(0, M, TAIL):
-                    score(c0)
-            if s == 4:
-                for c0 in range(0, M, BANK):
-                    quant_z(0, slice(c0, c0 + BANK), True)
+                    pair_copy(c0, 2, c0 // TAIL in TAIL_PAIR_SCALAR)
+                    quant_tail(c0)
+                    score_pass(1, c0)
+                    store(c0)
+            if s + 2 < 8:
+                place_product(s + 2)

@@ -17,345 +17,362 @@ ALU = mybir.AluOpType
 ACT = mybir.ActivationFunctionType
 
 P = 128
+PACK = 4
+K_PASS = P * PACK
 BANK = 512
-TAIL = 256
+GROUP = 16
+SLICES = H // P
+LAST = SLICES - 1
+AHEAD = 2
+W1_PIECE = 256
 
-FUSE_SCATTER = False
-FUSE_GATHER = True
-ZMUL_POOL = True
-TAIL_PAIR_SCALAR = (0, 1, 2)
-H_TAG = ("h0", "hsB", "hsA", "hsB", "hsA", "hsC", "hsA", "hsC")
-SIG_TAG = ("hsA", "hsB", "hsA", "hsC", "hsA", "hsC", "hsD", "hsC")
+CHUNK_WIDTHS = (256, 256, 256, 128, 128)
+CHUNKS_WOVEN_ON_SCALAR = 2
+
+H_BUFFER = ("h_first", "turn_odd", "turn_even", "h_third", "turn_even", "turn_odd", "turn_even", "turn_odd")
+X_BUFFER = ("w2_sum0", "w2_sum1", "turn_even", "turn_odd", "turn_even", "turn_odd", "w2_sum0", "turn_odd")
 
 
 def tile_list_vase_life_scores_kernel(
     tc, tab_words, tab_scales, offs, w1, w2_words, w2_scales, gain, offs2, wgs, offs3, wgt, cold, w3, out
 ):
     nc = tc.nc
+    chunks = [slice(sum(CHUNK_WIDTHS[:c]), sum(CHUNK_WIDTHS[: c + 1])) for c in range(len(CHUNK_WIDTHS))]
+    halves = [slice(0, BANK), slice(BANK, 2 * BANK)]
+
+    def entries(list_tile, cols):
+        return list_tile[:, cols.start // GROUP : cols.stop // GROUP]
+
+    def weave(copy, dst, src):
+        copy(out=dst.rearrange("p (c u) i -> p c i u", u=4), in_=src.rearrange("p i (c u) -> p c i u", u=4))
+
+    def load_scale_rows(engine, tile, rows):
+        for q in range(4):
+            engine.dma_start(
+                out=tile[32 * q : 32 * q + 4, :, :].bitcast(I32),
+                in_=rows[:, 4 * q : 4 * q + 4, :].rearrange("a r t -> r a t").bitcast(I32),
+            )
+
     with ExitStack() as ctx:
         keep = ctx.enter_context(tc.tile_pool(name="keep", bufs=1))
         ring = ctx.enter_context(tc.tile_pool(name="ring", bufs=2))
         psum = ctx.enter_context(tc.psum_pool(name="psum", bufs=8))
 
-        o1 = keep.tile([P, S // 16], U16, name="o1")
-        o2 = keep.tile([P, S // 16], U16, name="o2")
-        o3 = keep.tile([P, M // 16], U16, name="o3")
-        tabs = keep.tile([P, 2, T], U8, name="tabs")
-        w2s_raw = keep.tile([P, 2, H], U8, name="w2s_raw")
+        pick_list = keep.tile([P, S // GROUP], U16, name="pick_list")
+        put_list = keep.tile([P, S // GROUP], U16, name="put_list")
+        read_list = keep.tile([P, M // GROUP], U16, name="read_list")
+        tab_scale_sb = keep.tile([P, 2, T], U8, name="tab_scale_sb")
+        w2_scale_sb = keep.tile([P, 2, H], U8, name="w2_scale_sb")
         page = keep.tile([P, T2], F32, name="page")
-        gain_sb = keep.tile([P, 2, 4], F32, name="gain_sb")
+        gain_sb = keep.tile([P, 2, PACK], F32, name="gain_sb")
 
-        nc.vector.memset(tabs[:].rearrange("p a t -> p (a t)").bitcast(I32), 0)
-        nc.gpsimd.memset(w2s_raw[:].rearrange("p a t -> p (a t)").bitcast(I32), 0)
-
+        nc.vector.memset(tab_scale_sb[:].rearrange("p a t -> p (a t)").bitcast(I32), 0)
+        nc.gpsimd.memset(w2_scale_sb[:].rearrange("p a t -> p (a t)").bitcast(I32), 0)
         nc.vector.memset(page[:], 0.0)
 
         def load_w1(b):
-            raws = {}
+            pieces = {}
             for a in range(2):
-                for hf in range(2):
-                    raw = ring.tile([P, 4, 256], F32, name="w1raw", bufs=8)
+                for u in range(2):
+                    pieces[a, u] = ring.tile([P, PACK, W1_PIECE], F32, name="w1_piece", bufs=8)
+                    first = K_PASS * b + W1_PIECE * u
                     nc.sync.dma_start(
-                        out=raw[:],
-                        in_=w1[512 * a : 512 * (a + 1), 512 * b + 256 * hf : 512 * b + 256 * (hf + 1)].rearrange(
-                            "(p j) c -> p j c", j=4
+                        out=pieces[a, u][:],
+                        in_=w1[K_PASS * a : K_PASS * (a + 1), first : first + W1_PIECE].rearrange(
+                            "(p j) c -> p j c", j=PACK
                         ),
                     )
-                    raws[a, hf] = raw
-            return raws
+            return pieces
 
-        w1q = {}
-        w1s = {}
+        w1_codes = {}
+        w1_scale = {}
 
-        def quant_w1(b, raws):
-            codes = keep.tile([P, 2, 512], U32, name=("w1q0", "h0")[b], align_bytes=64)
+        def quantise_w1(b, pieces):
+            codes = keep.tile([P, 2, K_PASS], U32, name=("w1_codes0", "h_first")[b], align_bytes=64)
+            per_piece = W1_PIECE // PACK
             for a in range(2):
-                grp = ring.tile([P, 4, P, 4], BF16, name="w1grp", align_bytes=64)
-                for hf in range(2):
+                dealt = ring.tile([P, PACK, P, PACK], BF16, name="w1_dealt", align_bytes=64)
+                for u in range(2):
                     nc.scalar.copy(
-                        out=grp[:, :, 64 * hf : 64 * (hf + 1), :].rearrange("p t m j -> p m j t"),
-                        in_=raws[a, hf][:].rearrange("p j (m t) -> p m j t", t=4),
+                        out=dealt[:, :, per_piece * u : per_piece * (u + 1), :].rearrange("p i m j -> p m j i"),
+                        in_=pieces[a, u][:].rearrange("p j (m i) -> p m j i", i=PACK),
                     )
-                w1q[b, a] = codes[:, a, :]
-                w1s[b, a] = keep.tile([P, 512], U8, name=f"w1s{b}{a}", align_bytes=64)
+                w1_codes[b, a] = codes[:, a, :]
+                w1_scale[b, a] = keep.tile([P, K_PASS], U8, name=f"w1_scale{b}{a}", align_bytes=64)
                 nc.vector.quantize_mx(
-                    out=w1q[b, a].bitcast(FP8X4),
-                    scales=w1s[b, a][:],
-                    in_=grp[:].rearrange("p t m j -> p (t m j)"),
+                    out=w1_codes[b, a].bitcast(FP8X4),
+                    scales=w1_scale[b, a][:],
+                    in_=dealt[:].rearrange("p i m j -> p (i m j)"),
                 )
 
-        for q in range(4):
-            nc.gpsimd.dma_start(
-                out=w2s_raw[32 * q : 32 * q + 4, :, :].bitcast(I32),
-                in_=w2_scales[:, 4 * q : 4 * q + 4, :].rearrange("a r t -> r a t").bitcast(I32),
-            )
-        nc.sync.dma_start(o1[:], offs)
-        tabw = []
+        load_scale_rows(nc.gpsimd, w2_scale_sb, w2_scales)
+        nc.sync.dma_start(pick_list[:], offs)
+        tab_sb = []
         for a in range(2):
-            tw = keep.tile([P, T], U32, name=f"tabw{a}")
-            nc.sync.dma_start(out=tw[:].bitcast(I32), in_=tab_words[a].rearrange("p t i -> p (t i)").bitcast(I32))
-            tabw.append(tw)
-        for q in range(4):
-            nc.sync.dma_start(
-                out=tabs[32 * q : 32 * q + 4, :, :].bitcast(I32),
-                in_=tab_scales[:, 4 * q : 4 * q + 4, :].rearrange("a r t -> r a t").bitcast(I32),
-            )
-        w2w_raw = keep.tile([P, 2, 2 * H], U8, name="w2w_raw")
-        nc.sync.dma_start(out=w2w_raw[:].bitcast(I32), in_=w2_words.rearrange("a p c -> p a c").bitcast(I32))
-        raws0 = load_w1(0)
+            words = keep.tile([P, T], U32, name=f"tab_sb{a}")
+            nc.sync.dma_start(out=words[:].bitcast(I32), in_=tab_words[a].rearrange("p t i -> p (t i)").bitcast(I32))
+            tab_sb.append(words)
+        load_scale_rows(nc.sync, tab_scale_sb, tab_scales)
+        w2_sb = keep.tile([P, 2, 2 * H], U8, name="w2_sb")
+        nc.sync.dma_start(out=w2_sb[:].bitcast(I32), in_=w2_words.rearrange("a p c -> p a c").bitcast(I32))
+        w1_first = load_w1(0)
         wgs_sb = keep.tile([P, S], F32, name="wgs_sb")
-        nc.sync.dma_start(out=gain_sb[:], in_=gain.rearrange("(b p i) -> p b i", b=2, i=4))
+        nc.sync.dma_start(out=gain_sb[:], in_=gain.rearrange("(b p i) -> p b i", b=2, i=PACK))
         nc.sync.dma_start(out=wgs_sb[:], in_=wgs)
-        nc.sync.dma_start(o2[:], offs2)
+        nc.sync.dma_start(put_list[:], offs2)
         wgt_sb = keep.tile([P, M], F32, name="wgt_sb")
 
-        gs = {}
+        w2_codes = {}
+        w2_scale = {}
 
-        def gather_scales(hf):
-            for a in range(2):
-                gs[a, hf] = keep.tile([P, BANK], U8, name=f"gs{a}{hf}", align_bytes=64)
-                nc.vector.tensor_copy(gs[a, hf][:], tabs[:, a, :].indirect(o1[:, 32 * hf : 32 * (hf + 1)]))
-
-
-        w2w = {}
-        w2s = {}
-
-        def deal_w2(b):
-            w2w[b] = keep.tile([P, 2, 4, 2 * P], U8, name=f"w2w{b}", align_bytes=64)
+        def deal_w2_words(b):
+            w2_codes[b] = keep.tile([P, 2, PACK, 2 * P], U8, name=f"w2_codes{b}", align_bytes=64)
             nc.scalar.copy(
-                out=w2w[b][:].bitcast(U16).rearrange("p a t m -> p a m t"),
-                in_=w2w_raw[:, :, 1024 * b : 1024 * (b + 1)].bitcast(U16).rearrange("p a (m t) -> p a m t", t=4),
+                out=w2_codes[b][:].bitcast(U16).rearrange("p a i m -> p a m i"),
+                in_=w2_sb[:, :, 2 * K_PASS * b : 2 * K_PASS * (b + 1)]
+                .bitcast(U16)
+                .rearrange("p a (m i) -> p a m i", i=PACK),
             )
 
         def deal_w2_scales(b):
-            dealt = keep.tile([P, 4, 2, P], U8, name=("w2s0", "m0")[b], align_bytes=64)
-            for t in range(4):
-                w2s[b, t] = dealt[:, t, :, :]
-                nc.gpsimd.tensor_copy(out=w2s[b, t], in_=w2s_raw[:, :, 512 * b + t : 512 * (b + 1) : 4])
+            dealt = keep.tile([P, PACK, 2, P], U8, name=("w2_scale0", "top_first")[b], align_bytes=64)
+            for i in range(PACK):
+                w2_scale[b, i] = dealt[:, i, :, :]
+                nc.gpsimd.tensor_copy(
+                    out=w2_scale[b, i], in_=w2_scale_sb[:, :, K_PASS * b + i : K_PASS * (b + 1) : PACK]
+                )
 
-        deal_w2(0)
+        deal_w2_words(0)
         deal_w2_scales(0)
 
-        gw = {}
-        for hf in range(2):
+        v_codes = {}
+        v_scale = {}
+        for hf, cols in enumerate(halves):
             for a in range(2):
-                gw[a, hf] = keep.tile([P, BANK], U32, name=f"gw{a}{hf}", align_bytes=64)
-                nc.vector.tensor_copy(gw[a, hf][:], tabw[a][:].indirect(o1[:, 32 * hf : 32 * (hf + 1)]))
-            gather_scales(hf)
+                v_codes[a, hf] = keep.tile([P, BANK], U32, name=f"v_codes{a}{hf}", align_bytes=64)
+                nc.vector.tensor_copy(v_codes[a, hf][:], tab_sb[a][:].indirect(entries(pick_list, cols)))
+            for a in range(2):
+                v_scale[a, hf] = keep.tile([P, BANK], U8, name=f"v_scale{a}{hf}", align_bytes=64)
+                nc.vector.tensor_copy(v_scale[a, hf][:], tab_scale_sb[:, a, :].indirect(entries(pick_list, cols)))
             if hf == 0:
-                quant_w1(0, raws0)
+                quantise_w1(0, w1_first)
 
-        hs = {}
+        factor = {}
+        top = {}
+        w1_sum = {}
+        w2_sum = {}
+        placed = {}
 
-        def stage1(s):
-            b, t = divmod(s, 4)
-            wg = keep.tile([P, S], F32, name=f"wg{s % 2}")
-            nc.scalar.activation(out=wg[:], in_=wgs_sb[:], func=ACT.Copy, scale=gain_sb[:, b, t : t + 1])
+        def grade(s):
+            b, i = divmod(s, PACK)
+            factor[s] = keep.tile([P, S], F32, name=f"factor{s % 2}")
+            nc.scalar.activation(out=factor[s][:], in_=wgs_sb[:], func=ACT.Copy, scale=gain_sb[:, b, i : i + 1])
             if s == 0:
-                mh = keep.tile([P, S], F32, name="m0", align_bytes=64)
+                top[s] = keep.tile([P, S], F32, name="top_first", align_bytes=64)
             else:
-                mh = ring.tile([P, S], F32, name="mh")
-            b_sb = keep.tile([P, S], F32, name=f"bx{s % 2}")
-            for hf in range(2):
-                cols = slice(BANK * hf, BANK * (hf + 1))
-                acc_b = psum.tile([P, BANK], F32, name="bank")
+                top[s] = ring.tile([P, S], F32, name="top")
+            w2_sum[s] = keep.tile([P, S], F32, name=f"w2_sum{s % 2}", align_bytes=64)
+            for hf, cols in enumerate(halves):
+                w2_bank = psum.tile([P, BANK], F32, name="bank")
                 for a in range(2):
                     nc.tensor.matmul_mx(
-                        out=acc_b[:],
-                        lhsT=w2w[b][:, a, t, :].bitcast(FP4X4),
-                        lhsT_scale=w2s[b, t][:, a, :],
-                        rhs=gw[a, hf][:].bitcast(FP8X4),
-                        rhs_scale=gs[a, hf][:],
+                        out=w2_bank[:],
+                        lhsT=w2_codes[b][:, a, i, :].bitcast(FP4X4),
+                        lhsT_scale=w2_scale[b, i][:, a, :],
+                        rhs=v_codes[a, hf][:].bitcast(FP8X4),
+                        rhs_scale=v_scale[a, hf][:],
                         start=(a == 0),
                         stop=(a == 1),
                     )
-                acc_a = psum.tile([P, BANK], F32, name="bank")
+                w1_sum[s, hf] = psum.tile([P, BANK], F32, name="bank")
                 for a in range(2):
                     nc.tensor.matmul_mx(
-                        out=acc_a[:],
-                        lhsT=w1q[b, a][:, P * t : P * (t + 1)].bitcast(FP8X4),
-                        lhsT_scale=w1s[b, a][:, P * t : P * (t + 1)],
-                        rhs=gw[a, hf][:].bitcast(FP8X4),
-                        rhs_scale=gs[a, hf][:],
+                        out=w1_sum[s, hf][:],
+                        lhsT=w1_codes[b, a][:, P * i : P * (i + 1)].bitcast(FP8X4),
+                        lhsT_scale=w1_scale[b, a][:, P * i : P * (i + 1)],
+                        rhs=v_codes[a, hf][:].bitcast(FP8X4),
+                        rhs_scale=v_scale[a, hf][:],
                         start=(a == 0),
                         stop=(a == 1),
                     )
-                nc.scalar.copy(out=b_sb[:, cols], in_=acc_b[:])
-                nc.vector.tensor_tensor(mh[:, cols], acc_a[:], b_sb[:, cols], ALU.max)
-            hs[s] = (mh, wg)
+                nc.scalar.copy(out=w2_sum[s][:, cols], in_=w2_bank[:])
 
-        def place_product(s):
-            mh, wg = hs[s]
-            h = keep.tile([P, S], F32, name=H_TAG[s], align_bytes=64)
-            width = BANK if s == 0 else S
-            for c0 in range(0, S, width):
-                cols = slice(c0, c0 + width)
-                nc.gpsimd.tensor_tensor(h[:, cols], mh[:, cols], wg[:, cols], ALU.mult)
-            hs[s] = h
+        def take_max(s, hf):
+            nc.vector.tensor_tensor(top[s][:, halves[hf]], w1_sum[s, hf][:], w2_sum[s][:, halves[hf]], ALU.max)
 
-        def scatter(s):
-            width = BANK if s == 0 else S
-            for c0 in range(0, S, width):
-                window = page[:].indirect(o2[:, c0 // 16 : (c0 + width) // 16])
-                nc.vector.tensor_copy(window, hs[s][:, c0 : c0 + width])
+        def put_spans(s):
+            return halves if s == 0 else [slice(0, S)]
 
-        colds = {}
+        def weigh_for_page(s):
+            placed[s] = keep.tile([P, S], F32, name=H_BUFFER[s], align_bytes=64)
+            for cols in put_spans(s):
+                nc.gpsimd.tensor_tensor(placed[s][:, cols], top[s][:, cols], factor[s][:, cols], ALU.mult)
+
+        def put(s):
+            for cols in put_spans(s):
+                nc.vector.tensor_copy(page[:].indirect(entries(put_list, cols)), placed[s][:, cols])
+
+        cold_sb = {}
 
         def load_cold(s):
-            b, t = divmod(s, 4)
-            colds[s] = ring.tile([P, M], F32, name="cold_sb", bufs=2)
+            b, i = divmod(s, PACK)
+            cold_sb[s] = ring.tile([P, M], F32, name="cold_sb")
             nc.sync.dma_start(
-                out=colds[s][:], in_=cold[512 * b : 512 * (b + 1), :].rearrange("(p i) m -> p i m", i=4)[:, t, :]
+                out=cold_sb[s][:],
+                in_=cold[K_PASS * b : K_PASS * (b + 1), :].rearrange("(p i) m -> p i m", i=PACK)[:, i, :],
             )
 
-        zb = [keep.tile([P, 4, M], BF16, name=f"zb{b}") for b in range(2)]
+        z_rows = [keep.tile([P, PACK, M], BF16, name=f"z_rows{b}") for b in range(2)]
+        z_codes = {}
+        z_scale = {}
 
-        def read_page(s, x, sig, cols, last):
-            b, t = divmod(s, 4)
-            window = page[:].indirect(o3[:, cols.start // 16 : cols.stop // 16])
-            if FUSE_GATHER or last:
-                nc.vector.tensor_tensor(x[:, cols], window, wgt_sb[:, cols], ALU.mult)
-            else:
-                nc.vector.tensor_copy(x[:, cols], window)
-                picked = x
-                x = keep.tile([P, M], F32, name=f"wg{(s + 1) % 2}")
-                nc.gpsimd.tensor_tensor(x[:, cols], picked[:, cols], wgt_sb[:, cols], ALU.mult)
-            nc.scalar.activation(out=sig[:, cols], in_=x[:, cols], func=ACT.Sigmoid)
-
-        def weigh(s, sig, cols, last):
-            b, t = divmod(s, 4)
-            eng = nc.gpsimd if (ZMUL_POOL and not last) else nc.vector
-            eng.tensor_tensor(zb[b][:, t, cols], sig[:, cols], colds[s][:, cols], ALU.mult)
-
-        zq = {}
-
-        def quant_z(b, cols, on_scalar, codes0):
-            w = cols.stop - cols.start
-            zi = ring.tile([P, w, 4], BF16, name="zi", align_bytes=64)
-            dst = zi[:].rearrange("p (c i) t -> p c t i", i=4)
-            src = zb[b][:, :, cols].rearrange("p t (c i) -> p c t i", i=4)
-            if on_scalar:
-                nc.scalar.copy(out=dst, in_=src)
-            else:
-                nc.vector.tensor_copy(out=dst, in_=src)
-            codes = codes0[:, cols]
-            scales = keep.tile([P, w], U8, name=f"zs{b}_{cols.start}", align_bytes=64)
+        def quantise_z_first(hf, codes):
+            cols = halves[hf]
+            woven = ring.tile([P, BANK, PACK], BF16, name="z_woven", align_bytes=64)
+            weave(nc.scalar.copy, woven[:], z_rows[0][:, :, cols])
+            scale = keep.tile([P, BANK], U8, name=f"z_scale0{hf}", align_bytes=64)
             nc.vector.quantize_mx(
-                out=codes.bitcast(FP8X4), scales=scales[:], in_=zi[:].rearrange("p c t -> p (c t)")
+                out=codes[:, cols].bitcast(FP8X4), scales=scale[:], in_=woven[:].rearrange("p c i -> p (c i)")
             )
-            for c0 in range(cols.start, cols.stop, TAIL):
-                rel = slice(c0 - cols.start, c0 - cols.start + TAIL)
-                zq[b, c0] = (codes[:, rel], scales[:, rel])
+            for c, chunk in enumerate(chunks):
+                if cols.start <= chunk.start < cols.stop:
+                    z_codes[0, c] = codes[:, chunk]
+                    z_scale[0, c] = scale[:, chunk.start - cols.start : chunk.stop - cols.start]
 
-        zi1 = {}
+        z_woven_last = {}
 
-        def pair_copy(c0, first, on_scalar):
-            dst = zi1[c0][:, :, first : first + 2].rearrange("p (c i) t -> p c t i", i=4)
-            src = zb[1][:, first : first + 2, c0 : c0 + TAIL].rearrange("p t (c i) -> p c t i", i=4)
-            if on_scalar:
-                nc.scalar.copy(out=dst, in_=src)
-            else:
-                nc.vector.tensor_copy(out=dst, in_=src)
+        def weave_pair(copy, c, first):
+            weave(copy, z_woven_last[c][:, :, first : first + 2], z_rows[1][:, first : first + 2, chunks[c]])
 
-        def quant_tail(c0):
-            codes = keep.tile([P, TAIL], U32, name=f"zq1_{c0}", align_bytes=64)
-            scales = keep.tile([P, TAIL], U8, name=f"zs1_{c0}", align_bytes=64)
+        def quantise_z_last(c):
+            codes = keep.tile([P, CHUNK_WIDTHS[c]], U32, name=f"z_codes1{c}", align_bytes=64)
+            scale = keep.tile([P, CHUNK_WIDTHS[c]], U8, name=f"z_scale1{c}", align_bytes=64)
             nc.vector.quantize_mx(
-                out=codes[:].bitcast(FP8X4), scales=scales[:], in_=zi1[c0][:].rearrange("p c t -> p (c t)")
+                out=codes[:].bitcast(FP8X4), scales=scale[:], in_=z_woven_last[c][:].rearrange("p c i -> p (c i)")
             )
-            zq[1, c0] = (codes[:], scales[:])
+            z_codes[1, c] = codes[:]
+            z_scale[1, c] = scale[:]
 
-        w3g = {}
-        w3q = {}
-        w3s = {}
+        w3_woven = {}
+        w3_codes = {}
+        w3_scale = {}
 
-        def prep_w3(b):
-            raw = ring.tile([P, 4, N], F32, name="w3raw")
-            nc.sync.dma_start(out=raw[:], in_=w3[512 * b : 512 * (b + 1), :].rearrange("(p j) n -> p j n", j=4))
-            grp = ring.tile([P, N, 4], BF16, name="w3grp", align_bytes=64)
-            nc.scalar.copy(
-                out=grp[:].rearrange("p (c i) t -> p c t i", i=4),
-                in_=raw[:].rearrange("p t (c i) -> p c t i", i=4),
+        def cast_w3(b):
+            rows = ring.tile([P, PACK, N], F32, name="w3_rows")
+            nc.sync.dma_start(
+                out=rows[:], in_=w3[K_PASS * b : K_PASS * (b + 1), :].rearrange("(p j) n -> p j n", j=PACK)
             )
-            w3g[b] = grp
+            w3_woven[b] = ring.tile([P, N, PACK], BF16, name="w3_woven", align_bytes=64)
+            weave(nc.scalar.copy, w3_woven[b][:], rows[:])
 
-        def quant_w3():
-            codes = keep.tile([P, 2, N], U32, name="hsB", align_bytes=64)
+        def quantise_w3():
+            codes = keep.tile([P, 2, N], U32, name="h_third", align_bytes=64)
             for b in range(2):
-                w3q[b] = codes[:, b, :]
-                w3s[b] = keep.tile([P, N], U8, name=f"w3s{b}", align_bytes=64)
+                w3_codes[b] = codes[:, b, :]
+                w3_scale[b] = keep.tile([P, N], U8, name=f"w3_scale{b}", align_bytes=64)
                 nc.vector.quantize_mx(
-                    out=w3q[b].bitcast(FP8X4), scales=w3s[b][:], in_=w3g[b][:].rearrange("p c t -> p (c t)")
+                    out=w3_codes[b].bitcast(FP8X4),
+                    scales=w3_scale[b][:],
+                    in_=w3_woven[b][:].rearrange("p c i -> p (c i)"),
                 )
 
-        banks = {}
+        def bank_tiles(c):
+            per_bank = BANK // CHUNK_WIDTHS[c]
+            return [range(n, min(n + per_bank, N // P)) for n in range(0, N // P, per_bank)]
 
-        def score_pass(b, c0):
-            if b == 0:
-                banks[c0] = [psum.tile([P, BANK], F32, name="bank") for u in range(2)]
-            for n in range(3):
-                nc.tensor.matmul_mx(
-                    out=banks[c0][n // 2][:, TAIL * (n % 2) : TAIL * (n % 2 + 1)],
-                    lhsT=w3q[b][:, P * n : P * (n + 1)].bitcast(FP8X4),
-                    lhsT_scale=w3s[b][:, P * n : P * (n + 1)],
-                    rhs=zq[b, c0][0].bitcast(FP8X4),
-                    rhs_scale=zq[b, c0][1],
-                    start=(b == 0 and n != 1),
-                    stop=(b == 1 and n != 0),
+        score_banks = {}
+
+        def score_pass(b, c):
+            width = CHUNK_WIDTHS[c]
+            for u, tiles in enumerate(bank_tiles(c)):
+                if b == 0:
+                    score_banks[c, u] = psum.tile([P, BANK], F32, name="bank")
+                for n in tiles:
+                    nc.tensor.matmul_mx(
+                        out=score_banks[c, u][:, width * (n - tiles[0]) : width * (n - tiles[0] + 1)],
+                        lhsT=w3_codes[b][:, P * n : P * (n + 1)].bitcast(FP8X4),
+                        lhsT_scale=w3_scale[b][:, P * n : P * (n + 1)],
+                        rhs=z_codes[b, c].bitcast(FP8X4),
+                        rhs_scale=z_scale[b, c],
+                        start=(b == 0 and n == tiles[0]),
+                        stop=(b == 1 and n == tiles[-1]),
+                    )
+
+        def store(c):
+            width = CHUNK_WIDTHS[c]
+            groups = bank_tiles(c)
+            for u, tiles in enumerate(groups):
+                staged = ring.tile([P, len(tiles), width], F32, name="w1_piece", bufs=8)
+                very_last = c == len(chunks) - 1 and u == len(groups) - 1
+                copy = nc.vector.tensor_copy if very_last else nc.scalar.copy
+                copy(out=staged[:].rearrange("p n m -> p (n m)"), in_=score_banks[c, u][:, : width * len(tiles)])
+                nc.sync.dma_start(
+                    out=out.rearrange("(n p) m -> p n m", p=P)[:, tiles[0] : tiles[-1] + 1, chunks[c]], in_=staged[:]
                 )
 
-        def store(c0):
-            staged = ring.tile([P, 3, TAIL], F32, name="w1raw", bufs=8)
-            nc.scalar.copy(out=staged[:, 0:2, :].rearrange("p n m -> p (n m)"), in_=banks[c0][0][:])
-            if c0 + TAIL < M:
-                nc.scalar.copy(out=staged[:, 2, :], in_=banks[c0][1][:, 0:TAIL])
-            else:
-                nc.vector.tensor_copy(out=staged[:, 2, :], in_=banks[c0][1][:, 0:TAIL])
-            nc.sync.dma_start(out=out.rearrange("(n p) m -> p n m", p=P)[:, :, c0 : c0 + TAIL], in_=staged[:])
+        def read_last(picked, gate, c):
+            cols = chunks[c]
+            nc.vector.tensor_tensor(
+                picked[:, cols], page[:].indirect(entries(read_list, cols)), wgt_sb[:, cols], ALU.mult
+            )
+            nc.scalar.activation(out=gate[:, cols], in_=picked[:, cols], func=ACT.Sigmoid)
 
-        raws1 = load_w1(1)
-        nc.sync.dma_start(o3[:], offs3)
+        w1_second = load_w1(1)
+        nc.sync.dma_start(read_list[:], offs3)
         nc.sync.dma_start(out=wgt_sb[:], in_=wgt)
-        for s in range(2):
-            stage1(s)
-            place_product(s)
+        for s in range(AHEAD):
+            grade(s)
+            take_max(s, 0)
+            take_max(s, 1)
+            weigh_for_page(s)
         deal_w2_scales(1)
-        chunks = range(0, M, TAIL)
-        for s in range(8):
-            scatter(s)
+
+        for s in range(SLICES):
+            b, i = divmod(s, PACK)
+            coming = s + AHEAD
+            put(s)
             if s == 0:
-                quant_w1(1, raws1)
-                deal_w2(1)
-                prep_w3(0)
-                prep_w3(1)
-            if s == 3:
-                quant_w3()
-            if s == 6:
-                codes0 = keep.tile([P, M], U32, name="hsA", align_bytes=64)
-                for c0 in range(0, M, BANK):
-                    quant_z(0, slice(c0, c0 + BANK), True, codes0)
-                for c0 in chunks:
-                    zi1[c0] = keep.tile([P, TAIL, 4], BF16, name=f"zi1_{c0}", align_bytes=64)
-                    pair_copy(c0, 0, True)
-            if s + 2 < 8:
-                stage1(s + 2)
+                quantise_w1(1, w1_second)
+                deal_w2_words(1)
+                cast_w3(0)
+                cast_w3(1)
+            if H_BUFFER[s] == "h_third":
+                quantise_w3()
+            if s == LAST - 1:
+                z_codes_first = keep.tile([P, M], U32, name=H_BUFFER[s], align_bytes=64)
+                quantise_z_first(0, z_codes_first)
+                for c in range(len(chunks)):
+                    z_woven_last[c] = keep.tile([P, CHUNK_WIDTHS[c], PACK], BF16, name=f"z_woven1{c}", align_bytes=64)
+                    weave_pair(nc.scalar.copy, c, 0)
+            if coming < SLICES:
+                grade(coming)
+                take_max(coming, 0)
+                if s < AHEAD:
+                    take_max(coming, 1)
             load_cold(s)
-            x = keep.tile([P, M], F32, name=f"bx{s % 2}")
-            sig = keep.tile([P, M], F32, name=SIG_TAG[s], align_bytes=64)
-            if s < 7:
-                read_page(s, x, sig, slice(0, M), False)
-                weigh(s, sig, slice(0, M), False)
+            picked = keep.tile([P, M], F32, name=X_BUFFER[s], align_bytes=64)
+            gate = keep.tile([P, M], F32, name="gate")
+            if s < LAST:
+                nc.vector.tensor_copy(picked[:], page[:].indirect(read_list[:]))
+                x = keep.tile([P, M], F32, name="x")
+                nc.gpsimd.tensor_tensor(x[:], picked[:], wgt_sb[:], ALU.mult)
+                nc.scalar.activation(out=gate[:], in_=x[:], func=ACT.Sigmoid)
+                if AHEAD <= s and coming < SLICES:
+                    take_max(coming, 1)
+                if s == LAST - 1:
+                    quantise_z_first(1, z_codes_first)
+                nc.gpsimd.tensor_tensor(z_rows[b][:, i, :], gate[:], cold_sb[s][:], ALU.mult)
             else:
-                for c0 in chunks:
-                    score_pass(0, c0)
-                read_page(s, x, sig, slice(0, TAIL), True)
-                for c0 in chunks:
-                    if c0 + TAIL < M:
-                        read_page(s, x, sig, slice(c0 + TAIL, c0 + 2 * TAIL), True)
-                    weigh(s, sig, slice(c0, c0 + TAIL), True)
-                    pair_copy(c0, 2, c0 // TAIL in TAIL_PAIR_SCALAR)
-                    quant_tail(c0)
-                    score_pass(1, c0)
-                    store(c0)
-            if s + 2 < 8:
-                place_product(s + 2)
+                for c in range(len(chunks)):
+                    score_pass(0, c)
+                read_last(picked, gate, 0)
+                for c, cols in enumerate(chunks):
+                    if c + 1 < len(chunks):
+                        read_last(picked, gate, c + 1)
+                    nc.vector.tensor_tensor(z_rows[b][:, i, cols], gate[:, cols], cold_sb[s][:, cols], ALU.mult)
+                    weave_pair(nc.scalar.copy if c < CHUNKS_WOVEN_ON_SCALAR else nc.vector.tensor_copy, c, 2)
+                    quantise_z_last(c)
+                    score_pass(1, c)
+                    store(c)
+            if coming < SLICES:
+                weigh_for_page(coming)

from contextlib import ExitStack

import concourse.mybir as mybir

K, T, S, H, T2, M, N = 1024, 2048, 1024, 1024, 2048, 1024, 384
FLOPS = 2 * (2 * K * H * S + H * N * M)

F32 = mybir.dt.float32
BF16 = mybir.dt.bfloat16
I32 = mybir.dt.int32
U32 = mybir.dt.uint32
U16 = mybir.dt.uint16
U8 = mybir.dt.uint8
FP8X4 = mybir.dt.float8_e4m3fn_x4
FP4X4 = mybir.dt.float4_e2m1fn_x4
ALU = mybir.AluOpType
ACT = mybir.ActivationFunctionType

P = 128
PACK = 4
K_PASS = P * PACK
BANK = 512
GROUP = 16
SLICES = H // P
LAST = SLICES - 1
AHEAD = 2
W1_PIECE = 256

CHUNK_WIDTHS = (256, 256, 256, 128, 128)
CHUNKS_WOVEN_ON_SCALAR = 2

H_BUFFER = ("h_first", "turn_odd", "turn_even", "h_third", "turn_even", "turn_odd", "turn_even", "turn_odd")
X_BUFFER = ("w2_sum0", "w2_sum1", "turn_even", "turn_odd", "turn_even", "turn_odd", "w2_sum0", "turn_odd")


def tile_list_vase_life_scores_kernel(
    tc, tab_words, tab_scales, offs, w1, w2_words, w2_scales, gain, offs2, wgs, offs3, wgt, cold, w3, out
):
    nc = tc.nc
    chunks = [slice(sum(CHUNK_WIDTHS[:c]), sum(CHUNK_WIDTHS[: c + 1])) for c in range(len(CHUNK_WIDTHS))]
    halves = [slice(0, BANK), slice(BANK, 2 * BANK)]

    def entries(list_tile, cols):
        return list_tile[:, cols.start // GROUP : cols.stop // GROUP]

    def weave(copy, dst, src):
        copy(out=dst.rearrange("p (c u) i -> p c i u", u=4), in_=src.rearrange("p i (c u) -> p c i u", u=4))

    def load_scale_rows(engine, tile, rows):
        for q in range(4):
            engine.dma_start(
                out=tile[32 * q : 32 * q + 4, :, :].bitcast(I32),
                in_=rows[:, 4 * q : 4 * q + 4, :].rearrange("a r t -> r a t").bitcast(I32),
            )

    with ExitStack() as ctx:
        keep = ctx.enter_context(tc.tile_pool(name="keep", bufs=1))
        ring = ctx.enter_context(tc.tile_pool(name="ring", bufs=2))
        psum = ctx.enter_context(tc.psum_pool(name="psum", bufs=8))

        pick_list = keep.tile([P, S // GROUP], U16, name="pick_list")
        put_list = keep.tile([P, S // GROUP], U16, name="put_list")
        read_list = keep.tile([P, M // GROUP], U16, name="read_list")
        tab_scale_sb = keep.tile([P, 2, T], U8, name="tab_scale_sb")
        w2_scale_sb = keep.tile([P, 2, H], U8, name="w2_scale_sb")
        page = keep.tile([P, T2], F32, name="page")
        gain_sb = keep.tile([P, 2, PACK], F32, name="gain_sb")

        nc.vector.memset(tab_scale_sb[:].rearrange("p a t -> p (a t)").bitcast(I32), 0)
        nc.gpsimd.memset(w2_scale_sb[:].rearrange("p a t -> p (a t)").bitcast(I32), 0)
        nc.vector.memset(page[:], 0.0)

        def load_w1(b):
            pieces = {}
            for a in range(2):
                for u in range(2):
                    pieces[a, u] = ring.tile([P, PACK, W1_PIECE], F32, name="w1_piece", bufs=8)
                    first = K_PASS * b + W1_PIECE * u
                    nc.sync.dma_start(
                        out=pieces[a, u][:],
                        in_=w1[K_PASS * a : K_PASS * (a + 1), first : first + W1_PIECE].rearrange(
                            "(p j) c -> p j c", j=PACK
                        ),
                    )
            return pieces

        w1_codes = {}
        w1_scale = {}

        def quantise_w1(b, pieces):
            codes = keep.tile([P, 2, K_PASS], U32, name=("w1_codes0", "h_first")[b], align_bytes=64)
            per_piece = W1_PIECE // PACK
            for a in range(2):
                dealt = ring.tile([P, PACK, P, PACK], BF16, name="w1_dealt", align_bytes=64)
                for u in range(2):
                    nc.scalar.copy(
                        out=dealt[:, :, per_piece * u : per_piece * (u + 1), :].rearrange("p i m j -> p m j i"),
                        in_=pieces[a, u][:].rearrange("p j (m i) -> p m j i", i=PACK),
                    )
                w1_codes[b, a] = codes[:, a, :]
                w1_scale[b, a] = keep.tile([P, K_PASS], U8, name=f"w1_scale{b}{a}", align_bytes=64)
                nc.vector.quantize_mx(
                    out=w1_codes[b, a].bitcast(FP8X4),
                    scales=w1_scale[b, a][:],
                    in_=dealt[:].rearrange("p i m j -> p (i m j)"),
                )

        load_scale_rows(nc.gpsimd, w2_scale_sb, w2_scales)
        nc.sync.dma_start(pick_list[:], offs)
        tab_sb = []
        for a in range(2):
            words = keep.tile([P, T], U32, name=f"tab_sb{a}")
            nc.sync.dma_start(out=words[:].bitcast(I32), in_=tab_words[a].rearrange("p t i -> p (t i)").bitcast(I32))
            tab_sb.append(words)
        load_scale_rows(nc.sync, tab_scale_sb, tab_scales)
        w2_sb = keep.tile([P, 2, 2 * H], U8, name="w2_sb")
        nc.sync.dma_start(out=w2_sb[:].bitcast(I32), in_=w2_words.rearrange("a p c -> p a c").bitcast(I32))
        w1_first = load_w1(0)
        wgs_sb = keep.tile([P, S], F32, name="wgs_sb")
        nc.sync.dma_start(out=gain_sb[:], in_=gain.rearrange("(b p i) -> p b i", b=2, i=PACK))
        nc.sync.dma_start(out=wgs_sb[:], in_=wgs)
        nc.sync.dma_start(put_list[:], offs2)
        wgt_sb = keep.tile([P, M], F32, name="wgt_sb")

        w2_codes = {}
        w2_scale = {}

        def deal_w2_words(b):
            w2_codes[b] = keep.tile([P, 2, PACK, 2 * P], U8, name=f"w2_codes{b}", align_bytes=64)
            nc.scalar.copy(
                out=w2_codes[b][:].bitcast(U16).rearrange("p a i m -> p a m i"),
                in_=w2_sb[:, :, 2 * K_PASS * b : 2 * K_PASS * (b + 1)]
                .bitcast(U16)
                .rearrange("p a (m i) -> p a m i", i=PACK),
            )

        def deal_w2_scales(b):
            dealt = keep.tile([P, PACK, 2, P], U8, name=("w2_scale0", "top_first")[b], align_bytes=64)
            for i in range(PACK):
                w2_scale[b, i] = dealt[:, i, :, :]
                nc.gpsimd.tensor_copy(
                    out=w2_scale[b, i], in_=w2_scale_sb[:, :, K_PASS * b + i : K_PASS * (b + 1) : PACK]
                )

        deal_w2_words(0)
        deal_w2_scales(0)

        v_codes = {}
        v_scale = {}
        for hf, cols in enumerate(halves):
            for a in range(2):
                v_codes[a, hf] = keep.tile([P, BANK], U32, name=f"v_codes{a}{hf}", align_bytes=64)
                nc.vector.tensor_copy(v_codes[a, hf][:], tab_sb[a][:].indirect(entries(pick_list, cols)))
            for a in range(2):
                v_scale[a, hf] = keep.tile([P, BANK], U8, name=f"v_scale{a}{hf}", align_bytes=64)
                nc.vector.tensor_copy(v_scale[a, hf][:], tab_scale_sb[:, a, :].indirect(entries(pick_list, cols)))
            if hf == 0:
                quantise_w1(0, w1_first)

        factor = {}
        top = {}
        w1_sum = {}
        w2_sum = {}
        placed = {}

        def grade(s):
            b, i = divmod(s, PACK)
            factor[s] = keep.tile([P, S], F32, name=f"factor{s % 2}")
            nc.scalar.activation(out=factor[s][:], in_=wgs_sb[:], func=ACT.Copy, scale=gain_sb[:, b, i : i + 1])
            if s == 0:
                top[s] = keep.tile([P, S], F32, name="top_first", align_bytes=64)
            else:
                top[s] = ring.tile([P, S], F32, name="top")
            w2_sum[s] = keep.tile([P, S], F32, name=f"w2_sum{s % 2}", align_bytes=64)
            for hf, cols in enumerate(halves):
                w2_bank = psum.tile([P, BANK], F32, name="bank")
                for a in range(2):
                    nc.tensor.matmul_mx(
                        out=w2_bank[:],
                        lhsT=w2_codes[b][:, a, i, :].bitcast(FP4X4),
                        lhsT_scale=w2_scale[b, i][:, a, :],
                        rhs=v_codes[a, hf][:].bitcast(FP8X4),
                        rhs_scale=v_scale[a, hf][:],
                        start=(a == 0),
                        stop=(a == 1),
                    )
                w1_sum[s, hf] = psum.tile([P, BANK], F32, name="bank")
                for a in range(2):
                    nc.tensor.matmul_mx(
                        out=w1_sum[s, hf][:],
                        lhsT=w1_codes[b, a][:, P * i : P * (i + 1)].bitcast(FP8X4),
                        lhsT_scale=w1_scale[b, a][:, P * i : P * (i + 1)],
                        rhs=v_codes[a, hf][:].bitcast(FP8X4),
                        rhs_scale=v_scale[a, hf][:],
                        start=(a == 0),
                        stop=(a == 1),
                    )
                nc.scalar.copy(out=w2_sum[s][:, cols], in_=w2_bank[:])

        def take_max(s, hf):
            nc.vector.tensor_tensor(top[s][:, halves[hf]], w1_sum[s, hf][:], w2_sum[s][:, halves[hf]], ALU.max)

        def put_spans(s):
            return halves if s == 0 else [slice(0, S)]

        def weigh_for_page(s):
            placed[s] = keep.tile([P, S], F32, name=H_BUFFER[s], align_bytes=64)
            for cols in put_spans(s):
                nc.gpsimd.tensor_tensor(placed[s][:, cols], top[s][:, cols], factor[s][:, cols], ALU.mult)

        def put(s):
            for cols in put_spans(s):
                nc.vector.tensor_copy(page[:].indirect(entries(put_list, cols)), placed[s][:, cols])

        cold_sb = {}

        def load_cold(s):
            b, i = divmod(s, PACK)
            cold_sb[s] = ring.tile([P, M], F32, name="cold_sb")
            nc.sync.dma_start(
                out=cold_sb[s][:],
                in_=cold[K_PASS * b : K_PASS * (b + 1), :].rearrange("(p i) m -> p i m", i=PACK)[:, i, :],
            )

        z_rows = [keep.tile([P, PACK, M], BF16, name=f"z_rows{b}") for b in range(2)]
        z_codes = {}
        z_scale = {}

        def quantise_z_first(hf, codes):
            cols = halves[hf]
            woven = ring.tile([P, BANK, PACK], BF16, name="z_woven", align_bytes=64)
            weave(nc.scalar.copy, woven[:], z_rows[0][:, :, cols])
            scale = keep.tile([P, BANK], U8, name=f"z_scale0{hf}", align_bytes=64)
            nc.vector.quantize_mx(
                out=codes[:, cols].bitcast(FP8X4), scales=scale[:], in_=woven[:].rearrange("p c i -> p (c i)")
            )
            for c, chunk in enumerate(chunks):
                if cols.start <= chunk.start < cols.stop:
                    z_codes[0, c] = codes[:, chunk]
                    z_scale[0, c] = scale[:, chunk.start - cols.start : chunk.stop - cols.start]

        z_woven_last = {}

        def weave_pair(copy, c, first):
            weave(copy, z_woven_last[c][:, :, first : first + 2], z_rows[1][:, first : first + 2, chunks[c]])

        def quantise_z_last(c):
            codes = keep.tile([P, CHUNK_WIDTHS[c]], U32, name=f"z_codes1{c}", align_bytes=64)
            scale = keep.tile([P, CHUNK_WIDTHS[c]], U8, name=f"z_scale1{c}", align_bytes=64)
            nc.vector.quantize_mx(
                out=codes[:].bitcast(FP8X4), scales=scale[:], in_=z_woven_last[c][:].rearrange("p c i -> p (c i)")
            )
            z_codes[1, c] = codes[:]
            z_scale[1, c] = scale[:]

        w3_woven = {}
        w3_codes = {}
        w3_scale = {}

        def cast_w3(b):
            rows = ring.tile([P, PACK, N], F32, name="w3_rows")
            nc.sync.dma_start(
                out=rows[:], in_=w3[K_PASS * b : K_PASS * (b + 1), :].rearrange("(p j) n -> p j n", j=PACK)
            )
            w3_woven[b] = ring.tile([P, N, PACK], BF16, name="w3_woven", align_bytes=64)
            weave(nc.scalar.copy, w3_woven[b][:], rows[:])

        def quantise_w3():
            codes = keep.tile([P, 2, N], U32, name="h_third", align_bytes=64)
            for b in range(2):
                w3_codes[b] = codes[:, b, :]
                w3_scale[b] = keep.tile([P, N], U8, name=f"w3_scale{b}", align_bytes=64)
                nc.vector.quantize_mx(
                    out=w3_codes[b].bitcast(FP8X4),
                    scales=w3_scale[b][:],
                    in_=w3_woven[b][:].rearrange("p c i -> p (c i)"),
                )

        def bank_tiles(c):
            per_bank = BANK // CHUNK_WIDTHS[c]
            return [range(n, min(n + per_bank, N // P)) for n in range(0, N // P, per_bank)]

        score_banks = {}

        def score_pass(b, c):
            width = CHUNK_WIDTHS[c]
            for u, tiles in enumerate(bank_tiles(c)):
                if b == 0:
                    score_banks[c, u] = psum.tile([P, BANK], F32, name="bank")
                for n in tiles:
                    nc.tensor.matmul_mx(
                        out=score_banks[c, u][:, width * (n - tiles[0]) : width * (n - tiles[0] + 1)],
                        lhsT=w3_codes[b][:, P * n : P * (n + 1)].bitcast(FP8X4),
                        lhsT_scale=w3_scale[b][:, P * n : P * (n + 1)],
                        rhs=z_codes[b, c].bitcast(FP8X4),
                        rhs_scale=z_scale[b, c],
                        start=(b == 0 and n == tiles[0]),
                        stop=(b == 1 and n == tiles[-1]),
                    )

        def store(c):
            width = CHUNK_WIDTHS[c]
            groups = bank_tiles(c)
            for u, tiles in enumerate(groups):
                staged = ring.tile([P, len(tiles), width], F32, name="w1_piece", bufs=8)
                very_last = c == len(chunks) - 1 and u == len(groups) - 1
                copy = nc.vector.tensor_copy if very_last else nc.scalar.copy
                copy(out=staged[:].rearrange("p n m -> p (n m)"), in_=score_banks[c, u][:, : width * len(tiles)])
                nc.sync.dma_start(
                    out=out.rearrange("(n p) m -> p n m", p=P)[:, tiles[0] : tiles[-1] + 1, chunks[c]], in_=staged[:]
                )

        def read_last(picked, gate, c):
            cols = chunks[c]
            nc.vector.tensor_tensor(
                picked[:, cols], page[:].indirect(entries(read_list, cols)), wgt_sb[:, cols], ALU.mult
            )
            nc.scalar.activation(out=gate[:, cols], in_=picked[:, cols], func=ACT.Sigmoid)

        w1_second = load_w1(1)
        nc.sync.dma_start(read_list[:], offs3)
        nc.sync.dma_start(out=wgt_sb[:], in_=wgt)
        for s in range(AHEAD):
            grade(s)
            take_max(s, 0)
            take_max(s, 1)
            weigh_for_page(s)
        deal_w2_scales(1)

        for s in range(SLICES):
            b, i = divmod(s, PACK)
            coming = s + AHEAD
            put(s)
            if s == 0:
                quantise_w1(1, w1_second)
                deal_w2_words(1)
                cast_w3(0)
                cast_w3(1)
            if H_BUFFER[s] == "h_third":
                quantise_w3()
            if s == LAST - 1:
                z_codes_first = keep.tile([P, M], U32, name=H_BUFFER[s], align_bytes=64)
                quantise_z_first(0, z_codes_first)
                for c in range(len(chunks)):
                    z_woven_last[c] = keep.tile([P, CHUNK_WIDTHS[c], PACK], BF16, name=f"z_woven1{c}", align_bytes=64)
                    weave_pair(nc.scalar.copy, c, 0)
            if coming < SLICES:
                grade(coming)
                take_max(coming, 0)
                if s < AHEAD:
                    take_max(coming, 1)
            load_cold(s)
            picked = keep.tile([P, M], F32, name=X_BUFFER[s], align_bytes=64)
            gate = keep.tile([P, M], F32, name="gate")
            if s < LAST:
                nc.vector.tensor_copy(picked[:], page[:].indirect(read_list[:]))
                x = keep.tile([P, M], F32, name="x")
                nc.gpsimd.tensor_tensor(x[:], picked[:], wgt_sb[:], ALU.mult)
                nc.scalar.activation(out=gate[:], in_=x[:], func=ACT.Sigmoid)
                if AHEAD <= s and coming < SLICES:
                    take_max(coming, 1)
                if s == LAST - 1:
                    quantise_z_first(1, z_codes_first)
                nc.gpsimd.tensor_tensor(z_rows[b][:, i, :], gate[:], cold_sb[s][:], ALU.mult)
            else:
                for c in range(len(chunks)):
                    score_pass(0, c)
                read_last(picked, gate, 0)
                for c, cols in enumerate(chunks):
                    if c + 1 < len(chunks):
                        read_last(picked, gate, c + 1)
                    nc.vector.tensor_tensor(z_rows[b][:, i, cols], gate[:, cols], cold_sb[s][:, cols], ALU.mult)
                    weave_pair(nc.scalar.copy if c < CHUNKS_WOVEN_ON_SCALAR else nc.vector.tensor_copy, c, 2)
                    quantise_z_last(c)
                    score_pass(1, c)
                    store(c)
            if coming < SLICES:
                weigh_for_page(coming)
